import numpy as np
import ml_dtypes


def mxq(x, axis, fmt="e4m3"):
    dtype, down = {"e4m3": (ml_dtypes.float8_e4m3fn, 7), "e5m2": (ml_dtypes.float8_e5m2, 14)}[fmt]
    v = np.moveaxis(np.asarray(x, np.float32).astype(ml_dtypes.bfloat16).astype(np.float64), axis, -1)
    blocks = v.reshape(v.shape[:-1] + (-1, 32))
    amax = np.abs(blocks).max(-1, keepdims=True)
    byte = np.maximum(np.where(amax > 0, np.frexp(amax)[1] - 1 + 127, 0) - down, 1)
    scale = np.exp2(byte - 127.0)
    codes = (blocks / scale).astype(np.float32).astype(dtype).astype(np.float64)
    return np.moveaxis((codes * scale).reshape(v.shape), -1, axis)


WIDE = False


def mx_kscale(k):
    if not WIDE:
        return np.ones(k)
    levels = np.array([10, -10, 5, -5, 0])
    if k % 512:
        return np.exp2(np.random.permutation(np.resize(levels, k // 32))).repeat(32)
    a = np.empty((k // 512, 16))
    for p in range(k // 512):
        a[p, :8] = np.random.permutation(np.resize(levels, 8))
        for g in range(8):
            far = levels[np.abs(levels - a[p, g]) >= 10]
            a[p, g + 8] = far[np.random.randint(len(far))]
    return np.exp2(a.ravel()).repeat(32)


BF16 = ml_dtypes.bfloat16


def bf(x):
    return np.asarray(x, np.float32).astype(BF16)


def f64(x):
    return np.asarray(x).astype(np.float64)


E2M1 = np.array([0.0, 0.5, 1.0, 1.5, 2.0, 3.0, 4.0, 6.0, -0.0, -0.5, -1.0, -1.5, -2.0, -3.0, -4.0, -6.0])


def pack_weight(w, fmt):
    k, n = w.shape
    w = f64(bf(w)).reshape(k // 32, 32, n)
    amax = np.abs(w).max(1)
    if fmt == "e4m3":
        byte = np.frexp(amax)[1] - 1 + 127 - 7
    else:
        mant, ex = np.frexp(amax / 6.0)
        byte = np.where(mant > 0.5, ex, ex - 1) + 127
    byte = np.clip(np.where(amax > 0, byte, 1), 1, 254)
    scaled = (w * np.exp2(127.0 - byte)[:, None, :]).reshape(k, n).astype(np.float32)
    by_word = np.ascontiguousarray(scaled.reshape(k // 512, 128, 4, n).transpose(0, 1, 3, 2))
    if fmt == "e4m3":
        words = by_word.astype(ml_dtypes.float8_e4m3fn).view(np.uint8)
    else:
        c = by_word.astype(ml_dtypes.float4_e2m1fn).view(np.uint8) & 0xF
        words = c[..., 0::2] | (c[..., 1::2] << 4)
    return np.ascontiguousarray(words), np.ascontiguousarray(byte.astype(np.uint8).reshape(k // 512, 16, n))


def unpack_weight(words, scales, fmt):
    g, p, n, _ = words.shape
    if fmt == "e4m3":
        vals = np.ascontiguousarray(words).view(ml_dtypes.float8_e4m3fn).astype(np.float64)
    else:
        nib = np.empty((g, p, n, 4), np.uint8)
        nib[..., 0::2] = words & 0xF
        nib[..., 1::2] = words >> 4
        vals = E2M1[nib]
    vals = vals * np.repeat(np.exp2(scales.astype(np.float64) - 127.0), 8, axis=1)[..., None]
    return vals.transpose(0, 1, 3, 2).reshape(g * 512, n)
def pack4(w):
    words, scales = pack_weight(w, "e2m1")
    return words.reshape(words.shape[0], 128, -1), scales


def unpack4(words, scales):
    return unpack_weight(words.reshape(words.shape[0], 128, -1, 2), scales, "e2m1")


T, D, R = 2048, 1024, 512


def setup_inputs():
    s = mx_kscale(D)
    r = mx_kscale(T)
    c = mx_kscale(R)
    x = np.random.standard_normal((T, D)) * s * r[:, None]
    pos = np.random.standard_normal((T, R)) * r[:, None] * c
    keep = (1 + 0.1 * np.random.standard_normal(T)) / r
    gate = np.random.standard_normal((T, D))
    down = np.random.standard_normal((D, R)) / (3 * np.sqrt(D)) / s[:, None] * c
    mix = np.random.standard_normal((T, T)) / (3 * np.sqrt(T)) / r[:, None]
    up = np.random.standard_normal((R, D)) / np.sqrt(R) / c[:, None]
    down_words, down_scales = pack4(down)
    mix_words, mix_scales = pack4(mix)
    up_words, up_scales = pack4(up)
    return {"x": bf(x), "pos": bf(pos), "keep": bf(keep), "gate": bf(gate),
            "down_words": down_words, "down_scales": down_scales,
            "mix_words": mix_words, "mix_scales": mix_scales,
            "up_words": up_words, "up_scales": up_scales}


def reference(x, pos, keep, gate, down_words, down_scales, mix_words, mix_scales, up_words, up_scales):
    down = unpack4(down_words, down_scales)
    mix = unpack4(mix_words, mix_scales)
    up = unpack4(up_words, up_scales)
    u = f64(pos) + (mxq(f64(x), 1, "e4m3") @ down)
    v = f64(keep)[:, None] * u + (mix.T @ mxq(u, 0, "e4m3"))
    return (mxq(v, 1, "e4m3") @ up) / (1 + np.exp(-f64(gate)))

from contextlib import ExitStack

import concourse.mybir as mybir
from concourse.masks import make_identity

T, D, R = 2048, 1024, 512
FLOPS = 2 * T * D * R + 2 * T * T * R + 2 * T * R * D

F32 = mybir.dt.float32
BF16 = mybir.dt.bfloat16
I32 = mybir.dt.int32
U32 = mybir.dt.uint32
U8 = mybir.dt.uint8
FP8X4 = mybir.dt.float8_e4m3fn_x4
FP4X4 = mybir.dt.float4_e2m1fn_x4
ADD = mybir.AluOpType.add
MULT = mybir.AluOpType.mult
SIGMOID = mybir.ActivationFunctionType.Sigmoid

P = 128
EARLY_W = {5: [(0, 0)], 6: [(0, 1), (0, 2)], 7: [(0, 3), (1, 0)], 8: [(1, 1), (1, 2)], 9: [(1, 3), (2, 0)], 10: [(2, 1), (2, 2), (2, 3), (3, 0), (3, 1), (3, 2), (3, 3)]}
W_ON_VECTOR = {(2, 1), (2, 3), (3, 1)}
SG = (1, 3, 5, 7, 9, 11, 13, 14)
D_ON_SCALAR = {(0, 0), (1, 0), (2, 0), (3, 0)}
GROUPS = T // 512
BLOCKS = T // P


def tile_low_rank_row_mixer_t2_kernel(
    tc, x, pos, keep, gate, down_words, down_scales, mix_words, mix_scales, up_words, up_scales, out
):
    nc = tc.nc
    with ExitStack() as ctx:
        const = ctx.enter_context(tc.tile_pool(name="const", bufs=1))
        work = ctx.enter_context(tc.tile_pool(name="work", bufs=2))
        psum = ctx.enter_context(tc.psum_pool(name="psum", bufs=2))
        ctx.enter_context(tc.manual_schedule())

        def scale_plane(width, name):
            plane = const.tile([P, width], U8, name=name, align_bytes=64)
            nc.vector.memset(plane[:].bitcast(I32), 0)
            return plane

        def load_scales(queue, plane, scales, groups):
            src = scales.bitcast(I32).rearrange("g q n -> q g n")
            dst = plane[:].bitcast(I32).rearrange("p (g n) -> p g n", g=groups)
            for quad in range(4):
                queue.dma_start(out=dst[32 * quad : 32 * quad + 4], in_=src[4 * quad : 4 * quad + 4])

        down_sc = scale_plane(2 * R, "down_sc")
        load_scales(nc.sync, down_sc, down_scales, 2)
        warm = const.tile([P, 1], F32, name="warm")
        nc.vector.memset(warm[:], 0.0)
        nc.scalar.activation(warm[:], warm[:], SIGMOID)
        ident = const.tile([P, P], F32, name="ident")
        make_identity(nc, ident[:])

        mix_sc = scale_plane(4 * T, "mix_sc")
        up_sc = scale_plane(D, "up_sc")

        down_sb = const.tile([P, 2 * 2 * R], U8, name="down_sb", align_bytes=64)
        mix_sb = const.tile([P, 4 * 2 * T], U8, name="mix_sb", align_bytes=64)
        up_sb = const.tile([P, 2 * D], U8, name="up_sb", align_bytes=64)

        x_rows = x.rearrange("(g p t) k -> g p t k", p=P, t=4)
        pos_rows = pos.rearrange("(g p t) r -> g p t r", p=P, t=4)
        gate_rows = gate.rearrange("(q b p) c -> q p b c", p=P, b=4)

        x_sb = [work.tile([P, 4, D], BF16, name="x", bufs=3) for g in range(GROUPS)]
        pos_sb = [const.tile([P, 4, R], BF16, name="pos%d" % g) for g in range(GROUPS)]
        gate_sb = [const.tile([P, 4, D], BF16, name="gate%d" % q) for q in range(4)]

        keep_bf = const.tile([P, GROUPS, 4], BF16, name="keep_bf")
        nc.gpsimd.dma_start(out=keep_bf[:], in_=keep.rearrange("(g p t) -> p g t", p=P, t=4))
        keep_f = const.tile([P, GROUPS, 4], F32, name="keep_f")
        nc.gpsimd.tensor_copy(out=keep_f[:], in_=keep_bf[:])

        for t in range(4):
            nc.sync.dma_start(out=x_sb[0][:, t], in_=x_rows[0][:, t])
        nc.sync.dma_start(
            out=down_sb[:].bitcast(I32).rearrange("p (g n) -> p g n", g=2),
            in_=down_words.bitcast(I32).rearrange("g p n -> p g n"),
        )
        nc.sync.dma_start(out=pos_sb[0][:], in_=pos_rows[0])
        for g in range(1, GROUPS):
            for h in range(2):
                nc.sync.dma_start(out=x_sb[g][:, 2 * h : 2 * h + 2], in_=x_rows[g][:, 2 * h : 2 * h + 2])
            nc.sync.dma_start(out=pos_sb[g][:], in_=pos_rows[g])
        mix_dst = mix_sb[:].bitcast(I32).rearrange("p (g n) -> p g n", g=4)
        mix_src = mix_words.bitcast(I32).rearrange("g p n -> p g n")
        for h in range(2):
            nc.sync.dma_start(out=mix_dst[:, :, 512 * h : 512 * h + 512], in_=mix_src[:, :, 512 * h : 512 * h + 512])
        nc.sync.dma_start(
            out=up_sb[:].bitcast(I32),
            in_=up_words.bitcast(I32).rearrange("g p n -> p (g n)"),
        )
        load_scales(nc.sync, mix_sc, mix_scales, 4)
        load_scales(nc.sync, up_sc, up_scales, 1)
        for q in range(4):
            nc.sync.dma_start(out=gate_sb[q][:], in_=gate_rows[q])

        xt_banks, xg, xc, xs, s1_banks, u, w, ug, uc, us, w_t = {}, {}, {}, {}, {}, {}, {}, {}, {}, {}, {}

        def t_x(j):
            for tt in range(2):
                words = x_sb[j // 2][:, 2 * (j % 2) + tt].bitcast(F32)
                bank = psum.tile([P, 2, 2, P], F32, name="xt", tag="bank_a", bufs=3)
                for kc in range(2):
                    for half in range(2):
                        nc.tensor.transpose(bank[:, kc, half], words[:, 256 * kc + half : 256 * (kc + 1) : 2], ident[:])
                xt_banks[j, tt] = bank

        def a_x(j):
            xg[j] = work.tile([P, 2, 2 * P * 4], BF16, name="xg", bufs=3, align_bytes=64)
            for tt in range(2):
                nc.scalar.copy(
                    out=xg[j][:, tt].bitcast(F32).rearrange("p (k r u) -> p k r u", k=2, u=2),
                    in_=xt_banks[j, tt][:].rearrange("p k u r -> p k r u"),
                )

        def b_x(j):
            xc[j] = work.tile([P, 512], U32, name="xc", bufs=3, align_bytes=64)
            xs[j] = work.tile([P, 512], U8, name="xs", bufs=3, align_bytes=64)
            nc.vector.quantize_mx(
                out=xc[j][:].bitcast(FP8X4), scales=xs[j][:], in_=xg[j][:].rearrange("p a b -> p (a b)")
            )

        def stage1(j):
            for tt in range(2):
                bank = psum.tile([P, R], F32, name="s1", tag="bank_b", bufs=2)
                for kc in range(2):
                    cols = slice(256 * tt + 128 * kc, 256 * tt + 128 * kc + 128)
                    nc.tensor.matmul_mx(
                        out=bank[:],
                        lhsT=xc[j][:, cols].bitcast(FP8X4),
                        lhsT_scale=xs[j][:, cols],
                        rhs=down_sb[:, 2 * R * kc : 2 * R * (kc + 1)].bitcast(FP4X4),
                        rhs_scale=down_sc[:, R * kc : R * (kc + 1)],
                        start=(kc == 0),
                        stop=(kc == 1),
                    )
                s1_banks[j, tt] = bank

        def c_u(j):
            g = j // 2
            if j % 2 == 0:
                u[g] = work.tile([P, 4, R], F32, name="u", bufs=2)
                w[g] = work.tile([P, 4, R], F32, name="w", bufs=2)
            for tt in range(2):
                t = 2 * (j % 2) + tt
                nc.vector.tensor_tensor(
                    out=u[g][:, t].rearrange("p (a m) -> p a m", a=4),
                    in0=s1_banks[j, tt][:].rearrange("p (m a) -> p a m", a=4),
                    in1=pos_sb[g][:, t].rearrange("p (m a) -> p a m", a=4),
                    op=ADD,
                )
                if True:
                    nc.gpsimd.tensor_scalar(
                        out=w[g][:, t], in0=u[g][:, t], scalar1=keep_f[:, g, t : t + 1], scalar2=0.0, op0=MULT, op1=ADD
                    )

        def d_u(g):
            ug[g] = work.tile([P, R, 4], BF16, name="ug", bufs=2, align_bytes=64)
            src = u[g][:].rearrange("p t c -> p c t")
            for h in range(2):
                cols = slice(256 * h, 256 * h + 256)
                if (g, h) in D_ON_SCALAR:
                    nc.scalar.copy(out=ug[g][:, cols], in_=src[:, cols])
                else:
                    nc.vector.tensor_copy(out=ug[g][:, cols], in_=src[:, cols])

        def e_u(g):
            uc[g] = const.tile([P, R], U32, name="uc%d" % g, align_bytes=64)
            us[g] = const.tile([P, R], U8, name="us%d" % g, align_bytes=64)
            for h in (1, 0):
                cols = slice(256 * h, 256 * h + 256)
                nc.vector.quantize_mx(
                    out=uc[g][:, cols].bitcast(FP8X4),
                    scales=us[g][:, cols],
                    in_=ug[g][:, cols].rearrange("p c t -> p (c t)"),
                )

        def w_turn(g, a):
            if a == 0:
                w_t[g] = work.tile([P, 4, 512], F32, name="w_t", bufs=4)
            bank = psum.tile([P, 4, P], F32, name="wt", tag="bank_c", bufs=3)
            for t in range(4):
                nc.tensor.transpose(bank[:, t], w[g][:, t, P * a : P * (a + 1)], ident[:])
            copy = nc.vector.tensor_copy if (g, a) in W_ON_VECTOR else nc.scalar.copy
            copy(out=w_t[g][:, a].rearrange("m (p t) -> m p t", t=4), in_=bank[:].rearrange("m t p -> m p t"))

        def w_run(banks):
            for g, a in banks:
                w_turn(g, a)

        for j in range(10):
            g = (j - 3) // 2
            if j < 8:
                t_x(j)
            if 1 <= j < 9:
                stage1(j - 1)
            if j < 8:
                a_x(j)
            if j % 2 == 1 and g >= 0:
                d_u(g)
            w_run(EARLY_W.get(j, []))
            if j < 8:
                b_x(j)
            if 1 <= j < 9:
                c_u(j - 1)
            if j % 2 == 1 and g >= 0:
                e_u(g)
        w_run(EARLY_W[10])

        s2_banks, vg, vc, vs, s3_banks, sig = {}, {}, {}, {}, {}, {}

        def stage2(n):
            bank = psum.tile([P, 4, P], F32, name="s2", tag="bank_a", bufs=3)
            for a in range(4):
                for g in range(GROUPS):
                    cols = slice(P * a, P * (a + 1))
                    first = T * g + P * n
                    nc.tensor.matmul_mx(
                        out=bank[:, a],
                        lhsT=uc[g][:, cols].bitcast(FP8X4),
                        lhsT_scale=us[g][:, cols],
                        rhs=mix_sb[:, 2 * first : 2 * (first + P)].bitcast(FP4X4),
                        rhs_scale=mix_sc[:, first : first + P],
                        start=(g == 0),
                        stop=(g == GROUPS - 1),
                    )
            s2_banks[n] = bank

        def f_v(n):
            vg[n] = work.tile([P, P, 4], BF16, name="vg", bufs=3, align_bytes=64)
            col = P * (n % 4)
            nc.vector.tensor_tensor(
                out=vg[n][:],
                in0=s2_banks[n][:].rearrange("m a n -> m n a"),
                in1=w_t[n // 4][:, :, col : col + P].rearrange("m a n -> m n a"),
                op=ADD,
            )

        def h_v(n):
            vc[n] = work.tile([P, P], U32, name="vc", bufs=3, align_bytes=64)
            vs[n] = work.tile([P, P], U8, name="vs", bufs=3, align_bytes=64)
            nc.vector.quantize_mx(
                out=vc[n][:].bitcast(FP8X4), scales=vs[n][:], in_=vg[n][:].rearrange("m n a -> m (n a)")
            )

        def stage3(n):
            for h, tag, bufs in ((0, "bank_b", 2), (1, "bank_c", 3)):
                bank = psum.tile([P, 512], F32, name="s3", tag=tag, bufs=bufs)
                nc.tensor.matmul_mx(
                    out=bank[:],
                    lhsT=vc[n][:].bitcast(FP8X4),
                    lhsT_scale=vs[n][:],
                    rhs=up_sb[:, 1024 * h : 1024 * (h + 1)].bitcast(FP4X4),
                    rhs_scale=up_sc[:, 512 * h : 512 * (h + 1)],
                    start=True,
                    stop=True,
                )
                s3_banks[n, h] = bank

        def i_gate(n):
            sig[n] = work.tile([P, D], F32, name="sig", bufs=3)
            nc.scalar.activation(sig[n][:], gate_sb[n // 4][:, n % 4], SIGMOID)

        o_tiles = {}

        def j_out(n, h):
            if h == 0:
                o_tiles[n] = work.tile([P, D], F32, name="o", bufs=3)
            cols = slice(512 * h, 512 * (h + 1))
            if h == 1 and n in SG:
                z = work.tile([P, 512], F32, name="z", bufs=2)
                nc.scalar.copy(out=z[:], in_=s3_banks[n, h][:])
                nc.gpsimd.tensor_tensor(out=o_tiles[n][:, cols], in0=z[:], in1=sig[n][:, cols], op=MULT)
            else:
                nc.vector.tensor_tensor(out=o_tiles[n][:, cols], in0=s3_banks[n, h][:], in1=sig[n][:, cols], op=MULT)

        for n in range(BLOCKS + 1):
            if n < BLOCKS:
                stage2(n)
            if n >= 1:
                stage3(n - 1)
            if n < BLOCKS:
                i_gate(n)
                f_v(n)
            if n in (0, BLOCKS - 1) or n - 1 in SG:
                if n < BLOCKS:
                    h_v(n)
                if n >= 1:
                    j_out(n - 1, 0)
            else:
                j_out(n - 1, 0)
                if n < BLOCKS:
                    h_v(n)
            if n >= 1:
                j_out(n - 1, 1)
                nc.sync.dma_start(out=out[P * (n - 1) : P * n, :], in_=o_tiles[n - 1][:])
